import numpy as np, ml_dtypes
CORES = [6,15,38,47]
N = 4
BF = ml_dtypes.bfloat16
R, D, CAP, MEETS = 16, 4, 128, (1, 2)
L = R * 4 ** D; P = (4 * L - R) // 3; I = P - L
OFF = [(R * 4 ** t - R) // 3 for t in range(D + 2)]
NODE = np.arange(P)
def rebuild(v):
    for t in range(D - 1, -1, -1):
        k = v[..., OFF[t + 1]:OFF[t + 2]]
        v[..., OFF[t]:OFF[t + 1]] = (k[..., 0::4] + 3 * k[..., 1::4] + 5 * k[..., 2::4] + 7 * k[..., 3::4]) & 255
    return v
def places(kids):
    c = kids.reshape(N, 8, 4, P); pl = np.zeros((N, 8, P), np.int64); pl[..., :R] = np.arange(R)
    for t in range(D):
        k = np.take_along_axis(c, pl[:, :, None, OFF[t]:OFF[t + 1]], 3)
        pl[..., OFF[t + 1]:OFF[t + 2]] = k.transpose(0, 1, 3, 2).reshape(N, 8, -1)
    return pl
def logical(dg, pl):
    return np.take_along_axis(dg.astype(np.float32).astype(np.int32).reshape(N, 8, 16, P), pl[:, :, None], 3)
def opened(v, m):
    o = np.any(v != v[np.arange(N) ^ m], axis=2)
    for t in range(D):
        o[..., OFF[t + 1]:OFF[t + 2]] &= np.repeat(o[..., OFF[t]:OFF[t + 1]], 4, axis=-1)
    return o
def meet(v, m):
    o = opened(v, m); u = v[np.arange(N) ^ m]; w = v.copy()
    up = o[..., I:] & (u[:, :, 15, I:] > v[:, :, 15, I:])
    w[..., I:] = np.where(up[:, :, None], u[..., I:], v[..., I:])
    return rebuild(w)
def put(rng, v):
    pl = np.concatenate([np.broadcast_to(np.arange(R), (N, 8, R)), R + np.argsort(rng.random((N, 8, P - R)), axis=-1)], axis=-1)
    k = np.zeros((N, 8, 4, P), np.int32); np.put_along_axis(k, pl[:, :, None, :I], pl[..., R:].reshape(N, 8, I, 4).transpose(0, 1, 3, 2).astype(np.int32), 3)
    e = np.zeros((N, 8, 16, P), np.float32); np.put_along_axis(e, pl[:, :, None], v.astype(np.float32), 3)
    return {"dg": e.reshape(N, 128, P).astype(BF), "kids": k.reshape(N, 32, P)}
def whole(rng, *shape):
    return rng.integers(0, 256, shape, dtype=np.int32)
def pool(rng):
    par = np.argsort(rng.random((8, L // 4)), axis=1)[:, :CAP // 8]; m = np.zeros((8, L // 4, 4), bool); np.put_along_axis(m, par[:, :, None], True, 1)
    m = m.reshape(8, L); np.put_along_axis(m, np.argsort(rng.random((8, L)), axis=1)[:, :CAP // 2 - 2], True, 1); m[:, 0] = True; m[:, -1] = True
    return m, par
def change(rng, base, m, x):
    mod = m & (rng.random((N, 8, L)) < 0.6); one = rng.random((N, 8, 1, L)) < 0.3
    c = mod[:, :, None] & (~one | (np.arange(16)[:, None] == rng.integers(0, 16, (N, 8, 1, L))))
    c[:, :, 15] &= rng.random((N, 8, L)) >= 0.25
    return np.ascontiguousarray(np.where(c, x, base))
def collide(rng, base, x, par):
    k = np.take_along_axis(base.reshape(8, 16, L // 4, 4), par[:, None, :, None], 2); k = np.repeat(k[None], N, axis=0)
    e = rng.integers(1, 256, k.shape[:-1], dtype=np.int32); k[..., 0] = (k[..., 0] - 3 * e) & 255; k[..., 1] = (k[..., 1] + e) & 255
    w = x.reshape(N, 8, 16, L // 4, 4).copy(); np.put_along_axis(w, par[None, :, None, :, None], k, 3); return w.reshape(N, 8, 16, L)
def grow(rng, base, x, m, hide, own):
    v = np.zeros((N, 8, 16, P), np.int32); v[..., I:] = x; rebuild(v); b = np.zeros((8, 16, P), np.int32); b[..., I:] = base; rebuild(b)
    cl = np.zeros((8, P), bool); cl[:, I:] = m
    for t in range(D - 1, -1, -1):
        cl[:, OFF[t]:OFF[t + 1]] = np.any(cl[:, OFF[t + 1]:OFF[t + 2]].reshape(8, -1, 4), axis=2)
    h = cl & (rng.random((8, P)) < hide) & (NODE < I); v = np.where(h[:, None], b, v)
    o = cl & (rng.random((N, 8, P)) < own) & (NODE < I); v = np.where(o[:, :, None], whole(rng, N, 8, 16, P), v)
    s = ~cl & (rng.random((8, P)) < 0.02) & (NODE < I)
    return np.where(s[:, None], whole(rng, 8, 16, P), v)
def balance(rng, v, m):
    a = np.arange(16)[:, None]; low = (np.arange(N) < (np.arange(N) ^ MEETS[0]))[:, None, None, None]
    for t in range(D):
        n = R * 4 ** t; k = np.any(m.reshape(8, n, -1), axis=2)
        e = rng.integers(1, 32, (N, 8, 1, n)) * rng.choice(np.array([-1, 1]), (N, 8, 1, n))
        if t % 2 == 0:
            s = rng.integers(0, 16, (N, 8, 1, n)); c = 1 * (a == s) - 1 * (a == ((s + rng.integers(1, 16, (N, 8, 1, n))) & 15))
        else:
            s = rng.integers(0, 14, (N, 8, 1, n)); c = 1 * (a == s) - 2 * (a == s + 1) + 1 * (a == s + 2)
        z = rng.integers(64, 192, (8, 16, n)) + low * e * c
        v[..., OFF[t]:OFF[t + 1]] = np.where(k[:, None], z, v[..., OFF[t]:OFF[t + 1]])
    return v
def setup_inputs(rng):
    base = whole(rng, 8, 16, L); m, par = pool(rng); x = change(rng, base, m, whole(rng, N, 8, 16, L)); x = collide(rng, base, x, par[:, :CAP // 32])
    return put(rng, grow(rng, base, x, m, 0.1 * (NODE >= OFF[D - 1]), 0.05))
def setup_inputs_full(rng):
    base = whole(rng, 8, 16, L); m = np.zeros((8, L), bool); t = [t for t in range(D + 1) if R * 4 ** t >= CAP][0]; w = 4 ** (D - t)
    for i, g in enumerate(rng.permutation(8)):
        if i % 4 == 1: l = (4 * rng.permutation(L // 4)[:CAP // 4, None] + np.arange(4)).reshape(-1)
        elif i % 4 == 3: l = np.arange(L - CAP, L)
        else: l = rng.permutation(R * 4 ** t)[:CAP] * w + rng.integers(0, w, CAP)
        m[g, l] = True
    z = whole(rng, N, 8, 16, L)
    for s in (0, 15): z[:, :, s] = (z[0, :, s].copy() + 31 * np.arange(N)[:, None, None]) & 255
    v = grow(rng, base, np.where(m[:, None], z, base), m, 0.0, 0.0)
    return put(rng, balance(rng, v, m & (rng.random((8, L)) < 0.5)))
def setup_inputs_ties(rng):
    base = whole(rng, 8, 16, L); base[:, 15] = rng.choice(np.array([0, 1, 254, 255]), (8, L)); m, par = pool(rng)
    x = change(rng, base, m, whole(rng, N, 8, 16, L)); c = np.any(x != base, axis=2)
    x[:, :, 15] = np.where(c, np.clip(base[:, 15] + rng.choice(np.array([-1, 0, 0, 1]), (N, 8, L)), 0, 255), base[:, 15])
    return put(rng, grow(rng, base, x, m, 0.0, 0.05))
def setup_inputs_hidden(rng):
    base = whole(rng, 8, 16, L); m, par = pool(rng); x = change(rng, base, m, whole(rng, N, 8, 16, L)); x = collide(rng, base, x, par)
    return put(rng, grow(rng, base, x, m, 0.15, 0.3))
def setup_inputs_calm(rng):
    base = whole(rng, 8, 16, L); m, par = pool(rng); p = rng.permutation(8); a = int(rng.integers(0, N)); m[p[:5]] = False; m[p[3], 0] = True; m[p[4], -1] = True
    x = change(rng, base, m, whole(rng, N, 8, 16, L))
    for g, l in ((p[3], 0), (p[4], L - 1)):
        x[:, g, :, l] = base[g, :, l]; x[a ^ MEETS[1], g, :, l] = (base[g, :, l] + rng.integers(1, 256, 16)) & 255
    v = grow(rng, base, x, m, 0.0, 0.0); v[a ^ MEETS[0]] = v[a]; return put(rng, v)
def setup_inputs_spread(rng):
    def uneven(*shape):
        u = rng.random(shape, dtype=np.float32); u = u * u * u; u = np.minimum(256 * u * u, 255).astype(np.int32)
        return np.where(rng.random(shape, dtype=np.float32) < 0.1, np.int32(255), u)
    base = uneven(8, 16, L) * (rng.random((8, 1, L)) > 0.0625).astype(np.int32); m, par = pool(rng)
    x = change(rng, base, m, uneven(N, 8, 16, L)); x = collide(rng, base, x, par[:, :CAP // 32])
    return put(rng, grow(rng, base, x, m, 0.1 * (NODE >= OFF[D - 1]), 0.05))
def check_inputs(d):
    bad = []; v = d["dg"].astype(np.float32); k = d["kids"].astype(np.int64)
    if not (np.isfinite(v).all() and (v == np.floor(v)).all() and v.min() >= 0 and v.max() <= 255): bad.append("symbols")
    if k.min() < 0 or k.max() >= P: return bad + ["children"]
    pl = places(k)
    if (np.sort(pl, axis=-1) != NODE).any(): bad.append("places")
    elif np.take_along_axis(k.reshape(N, 8, 4, P), pl[:, :, None, I:], 3).any(): bad.append("leaves")
    if bad: return bad
    v = logical(d["dg"], pl)
    for m in MEETS:
        o = opened(v, m)
        if max(int(np.count_nonzero(o[..., OFF[t]:OFF[t + 1]], axis=-1).max()) for t in range(D + 1)) > CAP: return ["open nodes"]
        v = meet(v, m)
    return []
def reference(dg, kids):
    pl = places(kids); v = logical(dg, pl)
    for m in MEETS:
        v = meet(v, m)
    y = np.zeros((N, 8, 16, P), np.float32); np.put_along_axis(y, pl[:, :, None], v.astype(np.float32), 3)
    return {"y": y.reshape(N, 128, P).astype(BF)}

from concourse.mybir import AluOpType as ALU, ActivationFunctionType as ACT, AxisListType as AX

P = 5456
Q = P // 4
LEAFD = P
L3D = P + 512
WT = (1, 3, 5, 7)
W2 = sorted(set(a * b for a in WT for b in WT))
BIG = 8192.0
CFG = {"g0": (2, 2), "g7": (0, 2), "g1": (2, 1), "g2": (1, 2), "g3": (2, 0), "g4": (1, 1), "g5": (0, 0), "in3": 16,
       "pre3": 8, "nv1": 0, "nv2": 2, "f": (2, 1, 1, 3), "sf": (3, 0, 4), "lv2": 8}

BF, F32, I32, U16 = "bfloat16", "float32", "int32", "uint16"
_sb = {
    "KQ": (Q, I32), "DG": (P + 640, BF), "RT": (16, BF), "RRT": (16, BF),
    "PI": (1, I32), "CI": (8, I32), "COL": (16, BF), "COLF": (12, F32),
    "rC": (144, BF), "r16": (128, BF), "rG": (128, BF), "r4": (144, BF),
    "EQ4": (128, F32), "WKR": (128, F32), "KS": (128, F32), "SL": (128, F32),
    "WK": (144, F32), "WU3": (512, F32), "E": (8, F32), "ZR": (128, BF),
    "SI": (128 * 10, BF), "S2": (128 * 20, BF), "BLK": (128, BF), "TRI": (128, BF), "WF": (288, BF),
    "WC": (144, BF), "WD": (144, BF), "WV": (256, BF),
    "K4": (256, BF), "R4": (64, BF), "WP": (64, BF), "KW": (128, F32), "KW4": (128, F32), "R16": (128, F32),
    "SB": (8, F32), "ONE": (72, BF), "C256": (256, BF),
    "X1": (16, F32), "X2": (64, F32), "X3": (256, F32), "X4": (1152, F32), "MK": (1024, F32), "U3": (1152, F32),
    "AL1": (4, U16), "AL2": (16, U16), "AL3": (64, U16), "OL1": (4, U16), "OL2": (16, U16), "OL3": (64, U16),
    "PL1": (4, U16), "PL2": (16, U16), "PL3": (64, U16), "PL4": (256, U16), "TA": (64, F32), "TB": (64, F32),
    "UP": (320, BF), "RUP": (320, BF), "IN3": (1024, BF), "R3": (1024, BF),
    "NE0": (16, BF), "NEU": (320, BF), "NE3": (512, BF), "NE1": (128, BF),
    "FL": (288, BF), "CS": (80, F32), "GW": (72, F32), "JK": (8 * 72, BF), "ACC": (8, F32), "BL": (8, U16),
    "LE": (128, BF), "MB": (128, BF), "WR": (128, F32), "W4": (128, F32), "LS1": (8, U16), "LS2": (8, U16),
    "RL": (8, U16), "XC": (128, F32), "CL": (32, U16), "CG": (32, U16),
    "M1": (512, BF), "M2": (512, BF), "O1": (512, BF), "O2": (512, BF),
    "LV": (4608, BF), "UR": (1024, BF), "A3": (1152, BF), "B3": (1152, BF), "SG": (256, BF),
    "TK": (512, BF), "UU": (512, BF), "NR": (128, BF), "NL1": (128, BF), "NL2": (128, BF), "RN": (128, BF),
    "T1": (64, F32), "QI": (128, I32), "U2": (256, BF), "V2": (256, BF), "V1": (64, BF), "U1": (64, BF), "U0": (16, BF),
    "PM": (128, F32), "PS": (128, F32), "P3L": (8, U16),
}
SCRATCH = {k: ("sbuf", [128, n], d) for k, (n, d) in _sb.items()}
for _i in range(8):
    SCRATCH["PB%d" % _i] = ("psum", [128, 512], F32)
_MSG = ["RT", "UP", "I3", "I4", "M1", "LS", "A3", "A4", "NL", "M2"]
SEMAPHORES = ["cv", "cs", "ct", "cg", "ldk", "ldr", "ldd", "st"] + ["a" + m for m in _MSG] + ["l" + m for m in _MSG]


def emit(g, T, ops):
    que = {"v": g.vector, "s": g.scalar, "t": g.tensor, "g": g, "y": g.sync}
    lastw, readers, deps = {}, {}, []
    for n, (eng, fn, rd, wr, own) in enumerate(ops):
        d = set()
        for k in rd:
            if k in lastw:
                d.add(lastw[k])
            if k.startswith("PB"):
                d.update(m for m in readers.get(k, []) if ops[m][0] != eng)
        for k in wr:
            if k in lastw:
                d.add(lastw[k])
            d.update(readers.get(k, []))
        d.discard(n)
        if eng == "t":
            d = set(m for m in d if ops[m][0] != "t")
        deps.append(d)
        for k in rd:
            readers.setdefault(k, []).append(n)
        for k in wr:
            lastw[k] = n
            readers[k] = []
    needed = set()
    for n, d in enumerate(deps):
        for e in "vstg":
            ms = [m for m in d if ops[m][0] == e and ops[m][4] is None]
            if e == "t" and ms:
                ms = [max(ms)]
            needed.update(ms)
    count = {"v": 0, "s": 0, "t": 0, "g": 0}
    token, clock = {}, {}
    known = {e: {} for e in que}
    total = {}
    for n, (eng, fn, rd, wr, own) in enumerate(ops):
        if eng == "in":
            token[n] = own
            clock[n] = {own[0]: own[1]}
            total[own[0]] = own[1]
            continue
        kn = known[eng]
        for m in sorted(deps[n], reverse=True):
            if m not in token:
                continue
            s, v = token[m]
            if kn.get(s, 0) < v:
                que[eng].wait_ge(T.sem[s], v)
                for s2, v2 in clock[m].items():
                    if kn.get(s2, 0) < v2:
                        kn[s2] = v2
        ins = fn()
        if own is not None:
            token[n] = own
            if not own[0].startswith("l") or own[0].startswith("ld"):
                ins.then_inc(T.sem[own[0]], 16)
            total[own[0]] = own[1]
        elif n in needed:
            count[eng] += 1
            token[n] = ("c" + eng, count[eng])
            ins.then_inc(T.sem["c" + eng], 1)
            total["c" + eng] = count[eng]
        if n in token:
            clock[n] = dict(kn)
            clock[n][token[n][0]] = token[n][1]
    for s, v in total.items():
        if s != "st" and max(known[e].get(s, 0) for e in que) < v:
            g.wait_ge(T.sem[s], v)
    g.sync.wait_ge(T.sem["st"], total["st"])


def rank_program(g, core, T, topo):
    rank = T.rank_of(core)
    if rank is None:
        return
    peer1, peer2 = T.cores[rank ^ 1], T.cores[rank ^ 2]
    ops = []
    V, S, PE = g.vector, g.scalar, g.tensor
    PB = [T["PB%d" % i] for i in range(8)]

    def op(eng, fn, rd, wr, own=None):
        ops.append((eng, fn, list(rd), list(wr), own))

    def ts(out, in0, s1, s2, o0, o1, rd, wr):
        if o1 is None:
            op("v", lambda: V.tensor_scalar(out, in0, s1, None, o0), rd, wr)
        else:
            op("v", lambda: V.tensor_scalar(out, in0, s1, s2, o0, o1), rd, wr)

    def tt(out, a, b, o, rd, wr):
        op("v", lambda: V.tensor_tensor(out, a, b, o), rd, wr)

    def cp(out, a, rd, wr):
        op("v", lambda: V.tensor_copy(out, a), rd, wr)

    def scan(out, d0, d1, o0, o1, rd, wr):
        op("v", lambda: V.tensor_tensor_scan(out, d0, d1, 0.0, o0, o1), rd, wr)

    def act(out, a, rd, wr, func=ACT.Identity, bias=0.0, scale=1.0, acc=None):
        op("s", lambda: S.activation(out, a, func, bias=bias, scale=scale, accum_out=acc), rd, wr)

    def mm(out, w, x, st, sp, rd, bank):
        op("t", lambda: PE.matmul(out, w, x, st, sp), rd, ["PB%d" % bank])

    def iota(out, pat, base, cm, wr, flt=True):
        if flt:
            op("g", lambda: g.iota(out, pat, base, cm, allow_small_or_imprecise_dtypes=True), [], wr)
        else:
            op("g", lambda: g.iota(out, pat, base, cm), [], wr)

    def send(name, dst, src, peer, rd, wr):
        rid, pid, _ = topo.addr(peer)
        n = len(topo.engines(core, peer))
        op("g", lambda: g.remote_dma(dst, src, T.sem["a" + name], T.sem["l" + name], pid, rid, topo.mask(core, peer)),
           rd, [], ("l" + name, n))
        op("in", None, [], wr, ("a" + name, len(topo.engines(peer, core))))

    def blk(t, i, n=128):
        return t[:, i * n:(i + 1) * n]

    SIV = [1, 3, 5, 7, -1, -3, -5, -7, 129, 192]

    def si(w):
        return blk(T.SI, SIV.index(w))

    def s2(w):
        return blk(T.S2, W2.index(abs(w)) + (10 if w < 0 else 0))

    def make_s2(ws):
        for w in ws:
            op("g", lambda w=w: g.affine_select(s2(w), T.ZR[:], [[-1, 128]], ALU.not_equal, w / 256.0, 0, 1),
               ["ZR"], ["S2%d" % w])

    DGW = T.DG[:, 0:P + 640]
    DGK = ["DG", "DGd"]

    op("y", lambda: g.sync.dma_start(T.KQ[:], T.kids[:]), [], ["KQ"], ("ldk", 16))
    op("s", lambda: g.scalar.dma_start(T.RT[:], T.dg[:, 0:16]), [], ["RT"], ("ldr", 16))
    op("y", lambda: g.sync.dma_start(T.DG[:, 0:P], T.dg[:]), [], ["DG"], ("ldd", 16))

    iota(T.PI[:], [[0, 1]], 0, 1, ["PI"], False)
    iota(T.rC[:], [[1, 144]], -16, 0, ["rC"])
    iota(T.K4[:], [[0, 64], [-1, 4]], 1, 0, ["K4"])
    iota(T.rG[:], [[1, 8], [0, 16]], 0, 0, ["rG"])
    iota(T.r4[:], [[1, 36], [0, 4]], -4, 0, ["r4"])
    iota(T.r16[:], [[0, 8], [1, 16]], 0, 0, ["r16"])
    RC = T.rC[:, 16:144]
    sh, an = ALU.arith_shift_right, ALU.bitwise_and
    for j, (a, b) in enumerate([(0, 112), (0, 3), (4, 127), (0, 15), (1, 7), (0, 1), (3, 1), (2, 3)]):
        ts(T.CI[:, j:j + 1], T.PI[:], a, b, sh, an, ["PI"], ["CI%d" % j])
    cp(T.COL[:, 8:9], T.PI[:], ["PI"], ["COL8"])
    cp(T.COL[:, 0:8], T.CI[:], ["CI%d" % j for j in range(8)], ["COL"])

    def col(j):
        return T.COL[:, j:j + 1]

    def colf(j):
        return T.COLF[:, j:j + 1]

    def moved(t, s, c0=0):
        return t[:, c0 + 16 - s:c0 + 144 - s]

    eq = ALU.is_equal
    act(col(15), col(7), ["COL"], ["C15"], scale=-1.0, bias=1.0)
    ts(si(1), RC, col(8), None, eq, None, ["rC", "COL8"], ["SI1"])
    ts(T.BLK[:], T.rG[:], col(2), None, eq, None, ["rG", "COL"], ["BLK"])
    ts(T.E[:], T.rC[:, 16:24], col(1), None, eq, None, ["rC", "COL"], ["E"])
    ts(T.EQ4[:], T.K4[:, 0:128], col(15), None, eq, None, ["K4", "C15"], ["EQ4"])
    ts(colf(4), col(3), 15.0, None, eq, None, ["COL"], ["CF4"])
    tt(T.WKR[:], T.EQ4[:], T.BLK[:], ALU.mult, ["EQ4", "BLK"], ["WKR"])
    ts(T.WK[:], T.rC[:], col(0), col(7), ALU.subtract, eq, ["rC", "COL"], ["WK"])
    op("v", lambda: V.memset(T.DG[:, P:P + 640], 0.0), [], ["DGd"])
    act(colf(6), col(7), ["COL"], ["CF6"], scale=-BIG, bias=3 * BIG)
    act(colf(7), col(7), ["COL"], ["CF7"], scale=-BIG, bias=3 * BIG - (Q - 1) / 2.0)
    act(col(9), col(4), ["COL"], ["C9"], bias=col(0))
    act(col(10), col(5), ["COL"], ["C10"], scale=255.0, bias=1.0)
    act(col(11), col(5), ["COL"], ["C11"], scale=-255.0, bias=-1.0)
    act(col(13), col(2), ["COL"], ["C13"], scale=4.0)
    act(col(14), col(3), ["COL"], ["C14"], scale=-1.0, bias=-0.5)
    act(colf(8), col(7), ["COL"], ["CF8"], bias=float(LEAFD))
    act(T.KS[:], T.EQ4[:], ["EQ4"], ["KS"], scale=5 * BIG, bias=-BIG)
    act(T.SB[:], T.rC[:, 16:24], ["rC", "C14"], ["SB"], scale=-16.0, bias=col(14))
    act(colf(5), colf(4), ["CF4"], ["CF5"], scale=-1.0)
    act(T.X4[:, 1024:1152], RC, ["rC", "CF8"], ["X4d"], scale=4.0, bias=colf(8))
    act(T.KW4[:], T.EQ4[:], ["EQ4"], ["KW4"], scale=BIG)
    act(T.X4[:, 1024:1152], T.X4[:, 1024:1152], ["X4d", "E"], ["X4d"], scale=T.E[:, 0:1])
    send("RT", T.RRT[:], T.RT[:], peer1, ["RT"], ["RRT"])
    sfill = [lambda w=w: act(si(w), si(1), ["SI1"], ["SI%d" % w], scale=float(w)) for w in (-1, 3, 5, 7, 129)]
    sfill += [lambda h=h: act(blk(T.WV, h), T.BLK[:], ["BLK", "CF%d" % (4 + h)], ["WV%d" % h], scale=colf(4 + h))
              for h in range(2)]
    sfill += [lambda k=k: act(blk(T.WU3, k), T.BLK[:], ["BLK", "CF0"], ["WU3%d" % k], scale=colf(k)) for k in range(4)]
    sfill += [lambda w=w: act(si(w), si(1), ["SI1"], ["SI%d" % w], scale=float(w)) for w in (192, -3, -5, -7)]
    fill = [
        lambda: ts(T.WF[:, 0:144], T.rC[:], col(9), col(10), eq, ALU.mult, ["rC", "C9", "C10"], ["WF0"]),
        lambda: ts(T.WF[:, 144:288], T.rC[:], col(9), col(11), eq, ALU.mult, ["rC", "C9", "C11"], ["WF1"]),
        lambda: ts(T.WD[:], T.r4[:], col(13), None, eq, None, ["r4", "C13"], ["WD"]),
        lambda: ts(T.WC[:], T.rC[:], col(0), col(6), ALU.subtract, eq, ["rC", "COL"], ["WC"]),
        lambda: ts(T.TRI[:], RC, col(8), None, ALU.is_ge, None, ["rC", "COL8"], ["TRI"]),
        lambda: ts(T.COLF[:, 0:4], T.rC[:, 16:20], col(7), None, eq, None, ["rC", "COL"], ["CF0"]),
        lambda: tt(T.TRI[:], T.TRI[:], T.BLK[:], ALU.mult, ["TRI", "BLK"], ["TRI"]),
        lambda: ts(T.KW[:], T.r16[:], col(3), BIG, eq, ALU.mult, ["r16", "COL"], ["KW"]),
        lambda: ts(T.R4[:], T.K4[:, 0:64], 1.0, None, ALU.is_lt, None, ["K4"], ["R4"]),
        lambda: ts(T.R16[:], T.r16[:], 0.0, None, ALU.not_equal, None, ["r16"], ["R16"]),
    ]

    def fills(n, which=fill):
        for _ in range(min(n, len(which))):
            which.pop(0)()

    fills(CFG["f"][0])
    fills(CFG["sf"][2], sfill)

    def wrap(x, n, bank, c0, rd):
        for i in range(4):
            mm(PB[bank][:, c0:c0 + n // 4], moved(T.WK, 4 * i), x(i), i == 0, i == 3, rd + ["WK"], bank)

    def select(x, n, bank, rd):
        mm(PB[bank][:, 0:n], T.WKR[:], x, True, True, rd + ["WKR"], bank)
        return lambda: scan(T.SL[:, 0:n], T.KS[:, 0:n], PB[bank][:, 0:n], ALU.add, ALU.min, ["KS", "PB%d" % bank], ["SL"])

    def split(t, n, c, b, o1, o2):
        ts(T["AL%d" % t][:], c, o1, 1.0 / Q, ALU.add, ALU.mult, [b, "CF7"], ["AL%d" % t])
        ts(T.TA[:, 0:n], T["AL%d" % t][:], -float(Q), o2, ALU.mult, ALU.add, ["AL%d" % t, "CF6"], ["TA"])
        tt(T.TB[:, 0:n], c, T.TA[:, 0:n], ALU.add, [b, "TA"], ["TB"])
        cp(T["OL%d" % t][:], T.TB[:, 0:n], ["TB"], ["OL%d" % t])

    def listed(name, n):
        ts(T[name][:], T.SL[:, 3:n:4], colf(6), None, ALU.add, None, ["SL", "CF6"], [name])

    def mask(t, c0, n):
        act(T.MK[:, 16 * c0:16 * (c0 + n)], T.E[:].indirect(T["AL%d" % t][:, c0:c0 + n]), ["E", "AL%d" % t],
            ["MK%d" % c0])

    def children(t, x, c0, n, key):
        tt(x[:, 16 * c0:16 * (c0 + n)], T.KQ[:].indirect(T["OL%d" % t][:, c0:c0 + n]), T.MK[:, 16 * c0:16 * (c0 + n)],
           ALU.mult, ["KQ", "OL%d" % t, "MK%d" % c0], [key])

    ts(T.X1[:], T.KQ[:, 0:16], T.E[:, 0:1], None, ALU.mult, None, ["KQ", "E"], ["X1"])
    sel = select(T.X1[:], 16, 0, ["X1"])
    fills(CFG["f"][1])
    sel()
    split(1, 4, T.SL[:, 3:16:4], "SL", colf(7), colf(6))
    mask(1, 0, 4)
    fills(CFG["sf"][0], sfill)
    children(1, T.X2, 0, 4, "X2")
    sel = select(T.X2[:], 64, 5, ["X2"])
    listed("PL1", 16)
    fills(CFG["f"][2])
    sel()
    split(2, 16, T.SL[:, 3:64:4], "SL", colf(7), colf(6))
    mask(2, 0, 16)
    fills(CFG["sf"][1], sfill)
    children(2, T.X3, 0, 16, "X3")
    wrap(lambda i: T.X3[:, i::4], 256, 0, 0, ["X3"])
    listed("PL2", 64)
    act(T.UP[:, 0:64], DGW.indirect(T.PL1[:]), DGK + ["PL1"], ["UP1"])
    act(T.UP[:, 64:320], DGW.indirect(T.PL2[:]), DGK + ["PL2"], ["UP2"])
    send("UP", T.RUP[:], T.UP[:], peer1, ["UP1", "UP2"], ["RUP"])
    fills(CFG["f"][3])
    cp(T.PL3[:], PB[0][:, 0:64], ["PB0"], ["PL3"])
    n3 = CFG["in3"]
    for hf in range(2):
        a, b, c = 32 * hf, 32 * hf + n3, 32 * hf + 32
        cp(T.IN3[:, 16 * a:16 * b], DGW.indirect(T.PL3[:, a:b]), DGK + ["PL3"], ["IN3a%d" % hf])
        act(T.IN3[:, 16 * b:16 * c], DGW.indirect(T.PL3[:, b:c]), DGK + ["PL3"], ["IN3b%d" % hf])
        send("I%d" % (3 + hf), blk(T.R3, hf, 512), blk(T.IN3, hf, 512), peer1, ["IN3a%d" % hf, "IN3b%d" % hf],
             ["R3%d" % hf])
    iota(T.C256[:], [[0, 256]], 256, 0, ["C256"])
    iota(T.FL[:, 256:288], [[0, 32]], 1, 0, ["FLd"])
    iota(T.ONE[:], [[0, 72]], 1, 0, ["ONE"])
    iota(T.CS[:, 0:1], [[0, 1]], 0, 0, ["CS0"])
    iota(T.LV[:, 4096:4608], [[0, 512]], 0, 0, ["LVd"])
    iota(T.ZR[:], [[0, 128]], 0, 0, ["ZR"])
    iota(T.A3[:, 1024:1152], [[0, 128]], 0, 0, ["A3d"])
    iota(T.B3[:, 1024:1152], [[0, 128]], 0, 0, ["B3d"])
    iota(T.U3[:, 1024:1152], [[1, 128]], L3D, 0, ["U3d"])
    iota(T.WP[:], [[0, 16], [2, 4]], 1, 0, ["WP"])
    make_s2(W2[:7])

    def fold(x, sgn, rd):
        for hf in range(2):
            for h in range(2):
                mm(PB[3 + hf][:, 0:256], moved(T.WF, 8 * h, 144 * sgn), x[:, 512 * hf + h:512 * (hf + 1):2],
                   sgn == 0 and h == 0, sgn == 1 and h == 1, rd(hf) + ["WF%d" % sgn], 3 + hf)

    split(3, 64, PB[0][:, 0:64], "PB0", -(Q - 1) / 2.0, 0.0)
    fold(T.IN3, 0, lambda hf: ["IN3a%d" % hf, "IN3b%d" % hf])
    for c in range(4):
        mask(3, 16 * c, 16)
    for c in range(4):
        children(3, T.X4, 16 * c, 16, "X4%d" % c)
        bank = 5 if c < 2 else 0
        wrap(lambda i, c=c: T.X4[:, 256 * c + i:256 * (c + 1):4], 256, bank, 64 * (c % 2), ["X4%d" % c])
        if c == 2:
            cp(T.PL4[:, 0:128], PB[5][:, 0:128], ["PB5"], ["PL4a"])
            mm(PB[6][:, 0:320], si(1), T.UP[:], True, False, ["SI1", "UP1", "UP2"], 6)
            mm(PB[6][:, 0:320], si(-1), T.RUP[:], False, True, ["SI-1", "RUP"], 6)
    X4K = ["X4%d" % c for c in range(4)] + ["X4d"]
    nxt = [0]

    def leaves(gap):
        nv, ns = CFG[gap]
        for eng, n in (("s", ns), ("v", nv)):
            for _ in range(n):
                c = nxt[0]
                nxt[0] += 1
                src = DGW.indirect(T.PL4[:, 16 * c:16 * (c + 1)])
                rd = DGK + ["PL4a" if c < 8 else "PL4b"]
                (cp if eng == "v" else act)(blk(T.LV, c, 256), src, rd, ["LV%d" % c])

    LVK = ["LV%d" % c for c in range(16)] + ["LVd"]

    def wsum(out, bank, x, n, rd, first=True, last=True):
        if first:
            mm(out, si(129), T.C256[:, 0:n], True, False, ["SI129", "C256"], bank)
        for k in range(4):
            mm(out, si(WT[k]), x(k), False, last and k == 3, ["SI%d" % WT[k]] + rd, bank)

    def l3sum(j):
        bank = 1 + j // 2
        wsum(PB[bank][:, 256 * (j % 2):256 * (j % 2 + 1)], bank, lambda k: T.LV[:, 1024 * j + k:1024 * (j + 1):4], 256,
             LVK[4 * j:4 * j + 4])

    leaves("g0")
    act(T.NEU[:], PB[6][:, 0:320], ["PB6"], ["NEU"], ACT.Abs)
    leaves("g7")
    cp(T.PL4[:, 128:256], PB[0][:, 0:128], ["PB0"], ["PL4b"])
    tt(T.NE0[:], T.RT[:], T.RRT[:], ALU.not_equal, ["RT", "RRT"], ["NE0"])
    leaves("g1")

    def unwrapped(b, bank):
        for k in range(4):
            mm(PB[bank][:, k::4], blk(T.WU3, k), T.X3[:, 128 * b:128 * (b + 1)], True, True, ["X3", "WU3%d" % k], bank)

    def count_up(n0, n1, n2, k0, k1, k2):
        mm(PB[5][:, 1:256:4], T.BLK[:], n1, True, True, ["BLK", k1], 5)
        for k in range(4):
            mm(PB[5][:, 4 * k:256:16], T.BLK[:], n0, True, True, ["BLK", k0], 5)
        for i in range(4):
            mm(PB[5][:, 2:256:4], moved(T.WD, 4 * i), n2(i), i == 0, i == 3, ["WD", k2], 5)

    def count3():
        for u in range(8):
            mm(PB[5][:, 3:256:4], moved(T.WC, 2 * u), T.NE3[:, u::8], u == 0, u == 7, ["WC", "NE30", "NE31"], 5)

    def search(nv, gap3, gap4):
        scan(T.FL[:, 0:256], T.K4[:], PB[5][:, 0:256], ALU.max, ALU.min, ["K4", "PB5"], ["FL"])
        mm(PB[3][:, 0:72], T.BLK[:], T.FL[:, 3::4], True, True, ["BLK", "FL", "FLd"], 3)
        mm(PB[4][:, 0:72], T.TRI[:], T.FL[:, 3::4], True, True, ["TRI", "FL", "FLd"], 4)
        scan(T.CS[:, 1:73], T.ONE[:], PB[3][:, 0:72], ALU.mult, ALU.add, ["ONE", "PB3"], ["CS"])
        ns = 8 - nv
        for c in range(ns):
            act(blk(T.JK, c, 72), T.CS[:, 1:73], ["CS", "SB"], ["JK%d" % c, "ACC%d" % c], ACT.Sign,
                bias=T.SB[:, c:c + 1], acc=T.ACC[:, c:c + 1])
        for c in range(ns, 8):
            ts(blk(T.JK, c, 72), T.CS[:, 1:73], T.SB[:, c:c + 1], 0.0, ALU.add, ALU.is_lt, ["CS", "SB"], ["JK%d" % c])
        tt(T.GW[:], PB[4][:, 0:72], T.CS[:, 0:72], ALU.add, ["PB4", "CS", "CS0"], ["GW"])
        for c in range(ns, 8):
            op("v", lambda c=c: V.tensor_reduce(T.ACC[:, c:c + 1], blk(T.JK, c, 72), AX.X, ALU.add), ["JK%d" % c],
               ["ACC%d" % c])
        if nv:
            cp(T.BL[:, ns:8], T.ACC[:, ns:8], ["ACC%d" % c for c in range(ns, 8)], ["BLb"])
        gap3()
        ts(T.BL[:, 0:ns], T.ACC[:, 0:ns], -0.5, 36.0, ALU.mult, ALU.add, ["ACC%d" % c for c in range(ns)], ["BL"])
        tt(T.LE[:], T.GW[:].indirect(T.BL[:]), RC, ALU.is_le, ["GW", "BL", "BLb", "rC"], ["LE"])
        act(T.MB[:], RC.indirect(T.BL[:]), ["rC", "BL", "BLb"], ["MB"])
        mm(PB[3][:, 0:128], T.BLK[:], T.MB[:], True, False, ["BLK", "MB"], 3)
        mm(PB[3][:, 0:128], T.BLK[:], T.LE[:], False, True, ["BLK", "LE"], 3)
        gap4()

    def places(ls):
        scan(T.WR[:], T.KW[:], PB[3][:, 0:128], ALU.add, ALU.min, ["KW", "PB3"], ["WR"])
        cp(T[ls][:], T.WR[:, 15::16], ["WR"], [ls])
        cp(T.XC[:], T.X4[:].indirect(T[ls][:]), X4K + [ls], ["XC"])
        return select(T.XC[:], 128, 4, ["XC"])

    def pick(m, win, lst, rd):
        cp(T[m][:, 0:256], win.indirect(lst[:, 0:16]), rd, [m + "a"])
        act(T[m][:, 256:512], win.indirect(lst[:, 16:32]), rd, [m + "b"])

    def own_part(m):
        M, rd = T[m], [m + "a", m + "b"]
        mm(PB[5][:, 0:256], blk(T.WV, 1), M[:, 256:512], True, False, rd + ["WV1"], 5)
        mm(PB[6][:, 0:256], blk(T.WV, 1), M[:, 0:256], True, False, rd + ["WV1"], 6)
        mm(PB[7][:], si(-1), M[:], True, False, rd + ["SI-1"], 7)
        wsum(PB[0][:, 0:128], 0, lambda k: M[:, k::4], 128, rd, True, False)

    def take(o, between):
        mm(PB[5][:, 0:256], blk(T.WV, 0), T[o][:, 256:512], False, True, [o, "WV0"], 5)
        mm(PB[6][:, 0:256], blk(T.WV, 0), T[o][:, 0:256], False, True, [o, "WV0"], 6)
        mm(PB[7][:], si(1), T[o][:], False, True, [o, "SI1"], 7)
        act(T.SG[:], PB[5][:, 0:256], ["PB5"], ["SG"], ACT.Sign)
        act(T.TK[:, 256:512], T.SG[:], ["SG"], ["TKb"], ACT.Relu)
        ts(T.TK[:, 0:256], PB[6][:, 0:256], 0.0, None, ALU.is_gt, None, ["PB6"], ["TKa"])
        tt(T.UU[:, 0:256], PB[7][:, 0:256], T.TK[:, 0:256], ALU.mult, ["PB7", "TKa"], ["UUa"])
        tt(T.UU[:, 256:512], PB[7][:, 256:512], T.TK[:, 256:512], ALU.mult, ["PB7", "TKb"], ["UUb"])
        wsum(PB[0][:, 0:128], 0, lambda k: T.UU[:, k::4], 128, ["UUa", "UUb"], False, True)
        act(T.NR[:], PB[0][:, 0:128], ["PB0"], ["NR"], bias=-127.5)
        between()

    def put_leaves(m, a, b):
        tt(DGW.indirect(T.CL[:, a:b]), T[m][:, 16 * a:16 * b], T.UU[:, 16 * a:16 * b], ALU.add,
           [m + "a", m + "b", "UUa", "UUb", "CL"], DGK)

    def upper(x, sgn, rd):
        n = 0
        for a in range(4):
            for b in range(4):
                w = sgn * WT[a] * WT[b]
                mm(PB[2][:, 0:64], s2(w), x[:, 4 * a + b:1024:16], sgn > 0 and n == 0, sgn < 0 and n == 15,
                   rd + ["S2%d" % w], 2)
                n += 1
        if sgn > 0:
            mm(PB[1][:, 0:256], si(192), T.C256[:], True, False, ["SI192", "C256"], 1)
        for k in range(4):
            mm(PB[1][:, 0:256], si(sgn * WT[k]), x[:, k:1024:4], False, sgn < 0 and k == 3,
               rd + ["SI%d" % (sgn * WT[k])], 1)

    def nothing():
        pass

    count_up(T.NE0[:], T.NEU[:, 0:64], lambda i: T.NEU[:, 64 + i:320:4], "NE0", "NEU", "NEU")
    fold(T.R3, 1, lambda hf: ["R3%d" % hf])
    ts(T.NE3[:, 0:256], PB[3][:, 0:256], 0.0, None, ALU.not_equal, None, ["PB3"], ["NE30"])
    act(T.NE3[:, 256:512], PB[4][:, 0:256], ["PB4"], ["NE31"], ACT.Abs)
    count3()
    leaves("g2")
    search(CFG["nv1"], lambda: (l3sum(0), leaves("g3")), lambda: leaves("g4"))
    scan(T.W4[:], T.KW4[:], PB[3][:, 0:128], ALU.add, ALU.min, ["KW4", "PB3"], ["W4"])
    ts(T.CG[:], T.W4[:, 3::4], 4.0, col(1), ALU.mult, ALU.add, ["W4", "COL"], ["CG"])
    leaves("g5")
    pick("M1", T.LV[:], T.CG, LVK + ["CG"])
    send("M1", T.O1[:], T.M1[:], peer1, ["M1a", "M1b"], ["O1"])
    for j in (1, 2, 3):
        l3sum(j)
    act(T.UR[:, 0:512], PB[1][:], ["PB1"], ["URa"], bias=-127.5)
    tt(T.A3[:, 0:512], PB[1][:], T.UR[:, 0:512], ALU.subtract, ["PB1", "URa"], ["A3a"])
    send("A3", T.B3[:, 0:512], T.A3[:, 0:512], peer2, ["A3a"], ["B3a"])
    act(T.UR[:, 512:1024], PB[2][:], ["PB2"], ["URb"], bias=-127.5)
    tt(T.A3[:, 512:1024], PB[2][:], T.UR[:, 512:1024], ALU.subtract, ["PB2", "URb"], ["A3b"])
    send("A4", T.B3[:, 512:1024], T.A3[:, 512:1024], peer2, ["A3b"], ["B3b"])
    fills(len(sfill) - 4, sfill)
    own_part("M1")
    unwrapped(0, 1)
    fills(4, sfill)
    act(T.U3[:, 0:512], PB[1][:], ["PB1"], ["U3a"])
    fills(len(fill) - 2)
    sel = places("LS1")
    send("LS", T.RL[:], T.LS1[:], peer2, ["LS1"], ["RL"])
    make_s2(W2[7:] + [-w for w in W2[:2]])
    fills(2)
    sel()
    listed("CL", 128)
    A3K, B3K = ["A3a", "A3b", "A3d"], ["B3a", "B3b", "B3d"]
    take("O1", nothing)
    tt(T.NL1[:], PB[0][:, 0:128], T.NR[:], ALU.subtract, ["PB0", "NR"], ["NL1"])
    send("NL", T.RN[:], T.NL1[:], peer2, ["NL1"], ["RN"])
    make_s2([-w for w in W2[2:]])
    cp(T.A3[:].indirect(T.LS1[:]), T.NL1[:], ["NL1", "LS1"], A3K)
    upper(T.A3, 1, A3K)
    fold(T.A3, 0, lambda hf: A3K)
    unwrapped(1, 6)
    act(T.U3[:, 512:1024], PB[6][:], ["PB6"], ["U3b"])
    put_leaves("M1", 0, 32)
    p3 = CFG["pre3"]
    if p3:
        cp(DGW.indirect(T.PL3[:, 0:p3]), T.A3[:, 0:16 * p3], A3K + ["PL3"], DGK)

    cp(T.B3[:].indirect(T.RL[:]), T.RN[:], ["RN", "RL"], B3K)
    upper(T.B3, -1, B3K)
    fold(T.B3, 1, lambda hf: B3K)
    tt(T.T1[:], PB[2][:, 0:64], T.WP[:], ALU.mult, ["PB2", "WP"], ["T1"])
    scan(PB[2][:, 64:128], T.R4[:], T.T1[:], ALU.mult, ALU.add, ["R4", "T1"], ["PB2"])
    cp(T.QI[:], PB[2][:, 0:128], ["PB2"], ["QI"])
    act(T.U2[:], PB[1][:, 0:256], ["PB1"], ["U2"])
    tt(T.NE1[:], PB[2][:, 0:128], T.QI[:], ALU.not_equal, ["PB2", "QI"], ["NE1"])
    act(T.NE3[:, 0:256], PB[3][:, 0:256], ["PB3"], ["NE30"], ACT.Abs)
    tt(T.NEU[:, 0:256], PB[1][:, 0:256], T.U2[:], ALU.not_equal, ["PB1", "U2"], ["NEU"])
    act(T.NE3[:, 256:512], PB[4][:, 0:256], ["PB4"], ["NE31"], ACT.Abs)
    count_up(T.NE1[:, 67::4], T.NE1[:, 0:64], lambda i: T.NEU[:, i:256:4], "NE1", "NE1", "NEU")
    count3()
    search(CFG["nv2"], nothing, nothing)
    places("LS2")()
    listed("CL", 128)
    pick("M2", DGW, T.CL, DGK + ["CL"])
    send("M2", T.O2[:], T.M2[:], peer2, ["M2a", "M2b"], ["O2"])
    own_part("M2")
    tt(T.PM[:], T.U3[:].indirect(T.LS2[:]), T.KW[:], ALU.mult, ["U3a", "U3b", "U3d", "LS2", "KW"], ["PM"])
    scan(T.PS[:], T.R16[:], T.PM[:], ALU.mult, ALU.add, ["R16", "PM"], ["PS"])
    ts(T.P3L[:], T.PS[:, 15::16], 1.0 / BIG, None, ALU.mult, None, ["PS"], ["P3L"])
    cp(DGW.indirect(T.PL3[:, p3:64]), T.A3[:, 16 * p3:1024], A3K + ["PL3"], DGK)
    l2 = CFG["lv2"]
    take("O2", lambda: put_leaves("M2", 0, l2))
    tt(T.NL2[:], PB[0][:, 0:128], T.NR[:], ALU.subtract, ["PB0", "NR"], ["NL2"])
    cp(T.A3[:].indirect(T.LS2[:]), T.NL2[:], ["NL2", "LS2"], A3K)
    wsum(PB[1][:, 0:256], 1, lambda k: T.A3[:, k:1024:4], 256, A3K)
    act(T.U2[:], PB[1][:, 0:256], ["PB1"], ["U2"], bias=-127.5)
    put_leaves("M2", l2, 32)
    tt(T.V2[:], PB[1][:, 0:256], T.U2[:], ALU.subtract, ["PB1", "U2"], ["V2"])
    wsum(PB[2][:, 0:64], 2, lambda k: T.V2[:, k::4], 64, ["V2"])
    act(T.U1[:], PB[2][:, 0:64], ["PB2"], ["U1"], bias=-127.5)
    cp(DGW.indirect(T.P3L[:]), T.NL2[:], ["NL2", "P3L"], DGK)
    tt(T.V1[:], PB[2][:, 0:64], T.U1[:], ALU.subtract, ["PB2", "U1"], ["V1"])
    wsum(PB[3][:, 0:16], 3, lambda k: T.V1[:, k::4], 16, ["V1"])
    act(T.U0[:], PB[3][:, 0:16], ["PB3"], ["U0"], bias=-127.5)
    cp(DGW.indirect(T.PL2[:]), T.V2[:], ["V2", "PL2"], DGK)
    tt(T.DG[:, 0:16], PB[3][:, 0:16], T.U0[:], ALU.subtract, ["PB3", "U0"], DGK)
    cp(DGW.indirect(T.PL1[:]), T.V1[:], ["V1", "PL1"], DGK)
    op("y", lambda: g.sync.dma_start(T.y[:], T.DG[:, 0:P]), DGK, [], ("st", 16))
    emit(g, T, ops)
